import numpy as np
import ml_dtypes


def mxq(x, axis, fmt="e4m3"):
    dtype, down = {"e4m3": (ml_dtypes.float8_e4m3fn, 7), "e5m2": (ml_dtypes.float8_e5m2, 14)}[fmt]
    v = np.moveaxis(np.asarray(x, np.float32).astype(ml_dtypes.bfloat16).astype(np.float64), axis, -1)
    blocks = v.reshape(v.shape[:-1] + (-1, 32))
    amax = np.abs(blocks).max(-1, keepdims=True)
    byte = np.maximum(np.where(amax > 0, np.frexp(amax)[1] - 1 + 127, 0) - down, 1)
    scale = np.exp2(byte - 127.0)
    codes = (blocks / scale).astype(np.float32).astype(dtype).astype(np.float64)
    return np.moveaxis((codes * scale).reshape(v.shape), -1, axis)


WIDE = False


def mx_kscale(k):
    if not WIDE:
        return np.ones(k)
    levels = np.array([10, -10, 5, -5, 0])
    if k % 512:
        return np.exp2(np.random.permutation(np.resize(levels, k // 32))).repeat(32)
    a = np.empty((k // 512, 16))
    for p in range(k // 512):
        a[p, :8] = np.random.permutation(np.resize(levels, 8))
        for g in range(8):
            far = levels[np.abs(levels - a[p, g]) >= 10]
            a[p, g + 8] = far[np.random.randint(len(far))]
    return np.exp2(a.ravel()).repeat(32)


def f64(x):
    return np.asarray(x).astype(np.float64)


def striped(idx):
    return np.tile(idx.reshape(-1, 16).T, (8, 1)).astype(np.uint16)


def unstriped(offs):
    return offs[:16].T.reshape(-1).astype(np.int64)


E2M1 = np.array([0.0, 0.5, 1.0, 1.5, 2.0, 3.0, 4.0, 6.0, -0.0, -0.5, -1.0, -1.5, -2.0, -3.0, -4.0, -6.0])


def pack_weight(w, fmt):
    k, n = w.shape
    w = f64(np.asarray(w, np.float32).astype(ml_dtypes.bfloat16)).reshape(k // 32, 32, n)
    amax = np.abs(w).max(1)
    if fmt == "e4m3":
        byte = np.frexp(amax)[1] - 1 + 127 - 7
    else:
        mant, ex = np.frexp(amax / 6.0)
        byte = np.where(mant > 0.5, ex, ex - 1) + 127
    byte = np.clip(np.where(amax > 0, byte, 1), 1, 254)
    scaled = (w * np.exp2(127.0 - byte)[:, None, :]).reshape(k, n).astype(np.float32)
    by_word = np.ascontiguousarray(scaled.reshape(k // 512, 128, 4, n).transpose(0, 1, 3, 2))
    if fmt == "e4m3":
        words = by_word.astype(ml_dtypes.float8_e4m3fn).view(np.uint8)
    else:
        c = by_word.astype(ml_dtypes.float4_e2m1fn).view(np.uint8) & 0xF
        words = (c[..., 0::2] | (c[..., 1::2] << 4)).reshape(k // 512, 128, 2 * n)
    return np.ascontiguousarray(words), np.ascontiguousarray(byte.astype(np.uint8).reshape(k // 512, 16, n))


def unpack_weight(words, scales, fmt):
    g, _, n = scales.shape
    words = np.ascontiguousarray(words).reshape(g, 128, n, -1)
    if fmt == "e4m3":
        vals = words.view(ml_dtypes.float8_e4m3fn).astype(np.float64)
    else:
        nib = np.empty((g, 128, n, 4), np.uint8)
        nib[..., 0::2] = words & 0xF
        nib[..., 1::2] = words >> 4
        vals = E2M1[nib]
    vals = vals * np.repeat(np.exp2(scales.astype(np.float64) - 127.0), 8, axis=1)[..., None]
    return vals.transpose(0, 1, 3, 2).reshape(g * 512, n)


def gelu(v):
    return 0.5 * v * (1.0 + np.tanh(np.sqrt(2.0 / np.pi) * (v + 0.044715 * v**3)))


K, H, R, T, S, T2, S2, T3, P = 1024, 1024, 512, 2048, 512, 1024, 1024, 2048, 512

def setup_inputs():
    n = np.random.standard_normal
    s = mx_kscale(K)[:, None]
    u = s
    d = mx_kscale(R)[:, None]
    tab_words, tab_scales = pack_weight(n((K, T)) * s, "e4m3")
    tab2_words, tab2_scales = pack_weight(1.5 * n((H, T3)) / np.sqrt(H) / u, "e4m3")
    w2_words, w2_scales = pack_weight(n((K, R)) / np.sqrt(K) / s * d.T, "e2m1")
    return {
        "tab_words": tab_words, "tab_scales": tab_scales,
        "offs": striped(np.random.permutation(T)[:S]),
        "tab2_words": tab2_words, "tab2_scales": tab2_scales,
        "offs2": striped(np.random.permutation(T3)[:S2]),
        "offs3": striped(np.random.permutation(T2)[:S]),
        "offs4": striped(np.random.permutation(T2)[:P]),
        "w1": (n((K, R)) / np.sqrt(K) / s * d.T).astype(np.float32),
        "w2_words": w2_words, "w2_scales": w2_scales,
        "w3": (n((R, H)) / np.sqrt(R) / d).astype(np.float32),
        "gain": (np.exp(0.3 * n(H)) * u[:, 0]).astype(np.float32),
        "wgs": np.exp(0.3 * n((128, S))).astype(np.float32),
        "page0": (n((H, T2)) * u).astype(np.float32),
        "pm": np.exp(0.4 * n((H, P))).astype(np.float32),
        "dates": n((S2, P)).astype(np.float32)}

def reference(tab_words, tab_scales, offs, tab2_words, tab2_scales, offs2, offs3, offs4,
              w1, w2_words, w2_scales, w3, gain, wgs, page0, pm, dates):
    v = unpack_weight(tab_words, tab_scales, "e4m3")[:, unstriped(offs)]
    v2 = unpack_weight(tab2_words, tab2_scales, "e4m3")[:, unstriped(offs2)]
    y1 = mxq(f64(w1), 0, "e4m3").T @ v
    y2 = unpack_weight(w2_words, w2_scales, "e2m1").T @ v
    b = np.maximum(y1, y2)
    h = f64(gain)[:, None] * (mxq(f64(w3), 0, "e4m3").T @ mxq(b, 0, "e4m3"))
    page = f64(page0).copy()
    page[:, unstriped(offs3)] = np.tile(f64(wgs), (H // 128, 1)) * h
    x = page[:, unstriped(offs4)] * f64(pm)
    e = v2.T @ mxq(x, 0, "e4m3")
    f = v2.T @ v
    return e * np.tanh(f) + f64(dates)

@@ -1,0 +1,346 @@
+from contextlib import ExitStack
+
+import concourse.mybir as mybir
+
+K, H, R, T, S, T2, S2, T3, J = 1024, 1024, 512, 2048, 512, 1024, 1024, 2048, 512
+FLOPS = 2 * (2 * K * R * S + R * H * S + 2 * H * S2 * J)
+
+F32 = mybir.dt.float32
+BF16 = mybir.dt.bfloat16
+I32 = mybir.dt.int32
+U32 = mybir.dt.uint32
+U16 = mybir.dt.uint16
+U8 = mybir.dt.uint8
+FP8X4 = mybir.dt.float8_e4m3fn_x4
+FP4X4 = mybir.dt.float4_e2m1fn_x4
+MULT = mybir.AluOpType.mult
+ADD = mybir.AluOpType.add
+MAX = mybir.AluOpType.max
+COPY = mybir.ActivationFunctionType.Copy
+TANH = mybir.ActivationFunctionType.Tanh
+
+P = 128
+PACK = 4
+PASSES = 2
+BANK = 512
+CHUNK = 128
+HALF = 256
+GPSIMD_ADDS = 3
+GROUPED = [P, PACK, P, PACK]
+
+
+def tile_list_snapshot_finder_scores_kernel(
+    tc, tab_words, tab_scales, offs, tab2_words, tab2_scales, offs2, offs3, offs4,
+    w1, w2_words, w2_scales, w3, gain, wgs, page0, pm, dates, out,
+):
+    nc = tc.nc
+    with ExitStack() as ctx:
+        lists = ctx.enter_context(tc.tile_pool(name="lists", bufs=1))
+        keep = ctx.enter_context(tc.tile_pool(name="keep", bufs=1))
+        pair = ctx.enter_context(tc.tile_pool(name="pair", bufs=2))
+        ring = ctx.enter_context(tc.tile_pool(name="ring", bufs=3))
+        outs = ctx.enter_context(tc.tile_pool(name="outs", bufs=8))
+        psum = ctx.enter_context(tc.psum_pool(name="psum", bufs=1))
+
+        def kept(name, shape, dtype, tag=None):
+            return keep.tile(shape, dtype, name=name, tag=tag or name, align_bytes=64)
+
+        def bank(b):
+            return psum.tile([P, BANK], F32, name="bank%d" % b)
+
+        def load_list(name, src):
+            tile = lists.tile(list(src.shape), U16, name=name)
+            nc.sync.dma_start(tile[:], src)
+            return tile
+
+        def load_words(name, src):
+            tile = kept(name, [P, src.shape[1]], I32)
+            nc.sync.dma_start(tile[:], src.rearrange("p t i -> p (t i)").bitcast(I32))
+            return tile
+
+        def load_scales_side_by_side(queue, tile, src):
+            for q in range(4):
+                queue.dma_start(
+                    tile[32 * q : 32 * q + 4].bitcast(I32),
+                    src[:, 4 * q : 4 * q + 4, :].rearrange("a r n -> r a n").bitcast(I32),
+                )
+
+        def load_weight(tag, src):
+            tile = pair.tile([P, PACK, BANK], F32, name=tag, align_bytes=64)
+            nc.sync.dma_start(tile[:], src.rearrange("(p j) c -> p j c", j=PACK))
+            return tile
+
+        def quantize(codes, scales, values):
+            nc.vector.quantize_mx(out=codes.bitcast(FP8X4), scales=scales, in_=values)
+
+        def quantize_weight(name, grouped, raw, reuse=None):
+            nc.scalar.copy(
+                grouped[:].rearrange("p t m j -> p m j t"),
+                raw[:].rearrange("p j (m t) -> p m j t", t=PACK),
+            )
+            codes = kept(name + "_codes", [P, BANK], U32, reuse)
+            scales = kept(name + "_scales", [P, BANK], U8)
+            quantize(codes[:], scales[:], grouped[:].rearrange("p t m j -> p (t m j)"))
+            return codes, scales
+
+        tab_planes = kept("tab_planes", [P, PASSES, T], U8)
+        w2_planes = kept("w2_planes", [P, PASSES, R], U8)
+        tab2_planes = kept("tab2_planes", [P, T3], U8)
+        for planes in (w2_planes, tab_planes, tab2_planes):
+            flat = planes[:] if len(planes.shape) == 2 else planes[:].rearrange("p a n -> p (a n)")
+            nc.vector.memset(flat.bitcast(I32), 0)
+
+        sites = load_list("sites", offs)
+        snaps = load_list("snaps", offs2)
+        w2_raw = kept("w2_raw", [P, PASSES, 2 * R], U8)
+        nc.sync.dma_start(w2_raw[:].bitcast(I32), w2_words.rearrange("a p n -> p a n").bitcast(I32))
+        load_scales_side_by_side(nc.sync, w2_planes, w2_scales)
+        w1_raw = [load_weight("raw_a", w1[0:512, :])]
+        load_scales_side_by_side(nc.sync, tab_planes, tab_scales)
+        tab = [load_words("tab0", tab_words[0])]
+        w1_raw.append(load_weight("raw_a", w1[512:1024, :]))
+        for q in range(4):
+            nc.sync.dma_start(
+                tab2_planes[32 * q : 32 * q + 8, :].bitcast(I32),
+                tab2_scales[:, 4 * q : 4 * q + 4, :].bitcast(I32),
+            )
+        tab.append(load_words("tab1", tab_words[1]))
+        w3_raw = [load_weight("raw_b", w3[:, 0:512])]
+        tab2 = [load_words("tab2_0", tab2_words[0])]
+        slots = load_list("slots", offs3)
+        gains = kept("gains", [P, PASSES, PACK], F32)
+        nc.sync.dma_start(gains[:], gain.rearrange("(a p t) -> p a t", a=PASSES, t=PACK))
+        wgs_dealt = kept("wgs_dealt", [P, PACK, S], F32)
+        for q in (0, 2, 1, 3):
+            nc.sync.dma_start(wgs_dealt[32 * q : 32 * q + 32], wgs.rearrange("(p t) j -> p t j", t=PACK))
+
+        page_rows = page0.rearrange("(a p t) c -> a t p c", a=PASSES, t=PACK)
+        pm_rows = pm.rearrange("(a p t) c -> a p t c", a=PASSES, t=PACK)
+        pages, pms = [], []
+
+        def load_page():
+            i = len(pages)
+            tile = kept("page%d" % i, [P, T2], F32)
+            nc.sync.dma_start(tile[:], page_rows[i // PACK, i % PACK])
+            pages.append(tile)
+
+        def load_pm(n):
+            i = len(pms)
+            tile = kept("pm%d" % i, [P, n, J], F32)
+            nc.sync.dma_start(tile[:], pm_rows[i // PACK, :, i % PACK : i % PACK + n, :])
+            pms.extend([tile[:, u, :] for u in range(n)])
+
+        load_page()
+        load_page()
+        opened = load_list("opened", offs4)
+        load_pm(1)
+        w3_raw.append(load_weight("raw_b", w3[:, 512:1024]))
+        load_page()
+        load_pm(1)
+        for i in range(3, 7):
+            load_page()
+            load_pm(1)
+            if i == 3:
+                tab2.append(load_words("tab2_1", tab2_words[1]))
+        load_page()
+        load_pm(2)
+        dates_rows = dates.rearrange("(g m p) j -> g p m j", m=4, p=P)
+        dates_sb = []
+        for g in range(2):
+            tile = pair.tile([P, PACK, BANK], F32, name="raw_b", align_bytes=64)
+            nc.sync.dma_start(tile[:], dates_rows[g])
+            dates_sb.append(tile)
+
+        w2_codes = kept("w2_codes", [P, PASSES, PACK, 2 * P], U8)
+        w2_dealt = kept("w2_dealt", [P, PASSES, PACK, P], U8)
+        v_scales = [kept("v_scales%d" % a, [P, S], U8) for a in range(PASSES)]
+        v_codes = [kept("v_codes0", [P, S], U32)]
+        nc.vector.tensor_copy(
+            w2_codes[:].bitcast(U16),
+            w2_raw[:].bitcast(U16).rearrange("p a (m t) -> p a t m", t=PACK),
+        )
+        nc.vector.tensor_copy(w2_dealt[:], w2_planes[:].rearrange("p a (m t) -> p a t m", t=PACK))
+        for a in range(PASSES):
+            nc.vector.tensor_copy(v_scales[a][:], tab_planes[:, a, :].indirect(sites[:]))
+        w1_grouped0 = kept("w1_grouped0", GROUPED, BF16)
+        w1_q = [quantize_weight("w1_0", w1_grouped0, w1_raw[0], "tab_planes")]
+        nc.vector.tensor_copy(v_codes[0][:], tab[0][:].bitcast(U32).indirect(sites[:]))
+        v2_scales = kept("v2_scales", [P, S2], U8)
+        nc.vector.tensor_copy(v2_scales[:], tab2_planes[:].indirect(snaps[:]))
+        w1_q.append(quantize_weight("w1_1", kept("w1_grouped1", GROUPED, BF16), w1_raw[1], "tab2_planes"))
+        v_codes.append(kept("v_codes1", [P, S], U32, "w1_grouped1"))
+        for u in range(2):
+            nc.vector.tensor_copy(
+                v_codes[1][:, u * HALF : (u + 1) * HALF],
+                tab[1][:].bitcast(U32).indirect(sites[:, 16 * u : 16 * (u + 1)]),
+            )
+
+        n_chunks = S // CHUNK
+        y1 = [bank(c) for c in range(n_chunks)]
+        y2 = [bank(n_chunks + c) for c in range(n_chunks)]
+
+        def first_products(a, c, acc, weight, weight_scales):
+            cols = slice(c * CHUNK, (c + 1) * CHUNK)
+            for t in range(PACK):
+                nc.tensor.matmul_mx(
+                    out=acc[:, t * P : (t + 1) * P], lhsT=weight(a, t), lhsT_scale=weight_scales(a, t),
+                    rhs=v_codes[a][:, cols].bitcast(FP8X4), rhs_scale=v_scales[a][:, cols],
+                    start=(a == 0 and t == 0), stop=(a == PASSES - 1 and t == PACK - 1),
+                )
+
+        def w1_products(a, c):
+            first_products(
+                a, c, y1[c],
+                lambda a, t: w1_q[a][0][:, t * P : (t + 1) * P].bitcast(FP8X4),
+                lambda a, t: w1_q[a][1][:, t * P : (t + 1) * P],
+            )
+
+        def w2_products(a, c):
+            first_products(
+                a, c, y2[c], lambda a, t: w2_codes[:, a, t, :].bitcast(FP4X4), lambda a, t: w2_dealt[:, a, t, :]
+            )
+
+        for c in range(n_chunks):
+            w1_products(0, c)
+        for c in range(n_chunks):
+            w2_products(0, c)
+        for c in range(n_chunks):
+            w1_products(1, c)
+            w2_products(1, c)
+        b_codes = kept("b_codes", [P, S], U32)
+        b_scales = kept("b_scales", [P, S], U8)
+        b_grouped = []
+        w3_halves = [
+            w1_grouped0[:].rearrange("p t m j -> p (t m j)")[:, 0 : 2 * BANK],
+            kept("w3_grouped0", [P, 2 * BANK], BF16)[:],
+        ]
+        for c in range(n_chunks + 1):
+            if c < n_chunks:
+                if c in (1, 2):
+                    y1_sb = w3_halves[c - 1].bitcast(F32).rearrange("p (n t) -> p n t", t=PACK)
+                else:
+                    y1_sb = kept("y1_sb%d" % c, [P, CHUNK, PACK], F32)[:]
+                nc.scalar.copy(y1_sb, y1[c][:].rearrange("p (t n) -> p n t", t=PACK))
+                grouped = kept("b_grouped%d" % c, [P, CHUNK, PACK], BF16)
+                nc.vector.tensor_tensor(grouped[:], y2[c][:].rearrange("p (t n) -> p n t", t=PACK), y1_sb, MAX)
+                b_grouped.append(grouped)
+            if c > 0:
+                cols = slice((c - 1) * CHUNK, c * CHUNK)
+                quantize(b_codes[:, cols], b_scales[:, cols], b_grouped[c - 1][:].rearrange("p n t -> p (n t)"))
+
+
+        w3_q = [(kept("w3_0_codes", [P, BANK], U32), kept("w3_0_scales", [P, BANK], U8))]
+        for u in range(2):
+            nc.scalar.copy(
+                w3_halves[u].rearrange("p (t m j) -> p m j t", t=2, j=PACK),
+                w3_raw[0][:].rearrange("p j (m t) -> p m j t", t=PACK)[:, :, :, 2 * u : 2 * u + 2],
+            )
+            cols = slice(u * HALF, (u + 1) * HALF)
+            quantize(w3_q[0][0][:, cols], w3_q[0][1][:, cols], w3_halves[u])
+        v2_codes = [kept("v2_codes0", [P, S2], U32, "w1_grouped0")]
+
+        x_codes = [kept("x_codes%d" % a, [P, J], U32) for a in range(PASSES)]
+        x_scales = [kept("x_scales%d" % a, [P, J], U8) for a in range(PASSES)]
+
+        w3_grouped1 = kept("w3_grouped1", GROUPED, BF16)
+
+        def put(i):
+            a, t = divmod(i, PACK)
+            m = slice(t * P, (t + 1) * P)
+            acc = bank(i % 4)
+            nc.tensor.matmul_mx(
+                out=acc[:], lhsT=w3_q[a][0][:, m].bitcast(FP8X4), lhsT_scale=w3_q[a][1][:, m],
+                rhs=b_codes[:].bitcast(FP8X4), rhs_scale=b_scales[:], start=True, stop=True,
+            )
+            if i == 0:
+                h = w3_grouped1[:].rearrange("p t m j -> p (t m j)").bitcast(F32)[:, 0:S]
+            else:
+                h = ring.tile([P, S], F32, name="h")[:]
+            nc.scalar.activation(h, acc[:], COPY, scale=gains[:, a, t : t + 1])
+            nc.vector.tensor_tensor(pages[i][:].indirect(slots[:]), h, wgs_dealt[:, t, :], MULT)
+
+        def fetch(i, picked, cols):
+            nc.vector.tensor_tensor(
+                picked[:, i % PACK, :],
+                pages[i][:].indirect(opened[:, cols.start // 16 : cols.stop // 16]),
+                pms[i][:, cols], MULT,
+            )
+
+        def quantize_x(a, picked, cols):
+            grouped = kept("x_grouped%d_%d" % (a, cols.start), [P, cols.stop - cols.start, PACK], BF16)
+            nc.scalar.copy(
+                grouped[:].rearrange("p (c i) t -> p c t i", i=4),
+                picked[:].rearrange("p t (c i) -> p c t i", i=4),
+            )
+            quantize(x_codes[a][:, cols], x_scales[a][:, cols], grouped[:].rearrange("p n t -> p (n t)"))
+
+        whole = slice(0, J)
+        halves = [slice(0, HALF), slice(HALF, J)]
+        picked0 = pair.tile([P, PACK, J], F32, name="raw_a", align_bytes=64)
+        picked1 = [kept("picked1_%d" % u, [P, PACK, HALF], F32) for u in range(2)]
+        nc.vector.tensor_copy(v2_codes[0][:], tab2[0][:].bitcast(U32).indirect(snaps[:]))
+        put(0)
+        put(1)
+        fetch(0, picked0, whole)
+        w3_q.append(quantize_weight("w3_1", w3_grouped1, w3_raw[1]))
+        put(2)
+        fetch(1, picked0, whole)
+        v2_codes.append(kept("v2_codes1", [P, S2], U32))
+        nc.vector.tensor_copy(v2_codes[1][:], tab2[1][:].bitcast(U32).indirect(snaps[:]))
+        put(3)
+        fetch(2, picked0, whole)
+
+        tanh_f = kept("tanh_f", [P, S2 // P, J], F32)
+        for mt in range(S2 // P):
+            m = slice(mt * P, (mt + 1) * P)
+            acc = bank(4 + mt % 4)
+            for a in range(PASSES):
+                nc.tensor.matmul_mx(
+                    out=acc[:], lhsT=v2_codes[a][:, m].bitcast(FP8X4), lhsT_scale=v2_scales[4 * a :, m],
+                    rhs=v_codes[a][:].bitcast(FP8X4), rhs_scale=v_scales[a][:],
+                    start=(a == 0), stop=(a == PASSES - 1),
+                )
+            nc.scalar.activation(tanh_f[:, mt, :], acc[:], TANH)
+
+        put(4)
+        fetch(3, picked0, whole)
+        quantize_x(0, picked0, whole)
+        for i in (5, 6):
+            put(i)
+            for u in range(2):
+                fetch(i - 1, picked1[u], halves[u])
+        put(7)
+        for u in range(2):
+            fetch(6, picked1[u], halves[u])
+            fetch(7, picked1[u], halves[u])
+            quantize_x(1, picked1[u], halves[u])
+
+        out_rows = out.rearrange("(m p) j -> p m j", p=P)
+        e = [bank(b) for b in range(8)]
+        for a in range(PASSES):
+            for b in range(8):
+                cols = halves[b // 4]
+                for w in range(2):
+                    mt = 2 * (b % 4) + w
+                    m = slice(mt * P, (mt + 1) * P)
+                    nc.tensor.matmul_mx(
+                        out=e[b][:, w * HALF : (w + 1) * HALF],
+                        lhsT=v2_codes[a][:, m].bitcast(FP8X4), lhsT_scale=v2_scales[4 * a :, m],
+                        rhs=x_codes[a][:, cols].bitcast(FP8X4), rhs_scale=x_scales[a][:, cols],
+                        start=(a == 0 and w == 0), stop=(a == PASSES - 1 and w == 1),
+                    )
+        results = []
+        for b in range(8):
+            cols = halves[b // 4]
+            mt = 2 * (b % 4)
+            result = outs.tile([P, 2, HALF], F32, name="result")
+            nc.vector.tensor_tensor(
+                result[:], e[b][:].rearrange("p (w n) -> p w n", w=2), tanh_f[:, mt : mt + 2, cols], MULT
+            )
+            results.append(result)
+        for b in range(8):
+            cols = halves[b // 4]
+            mt = 2 * (b % 4)
+            engine = nc.gpsimd if b < GPSIMD_ADDS else nc.vector
+            engine.tensor_tensor(results[b][:], results[b][:], dates_sb[mt // 4][:, mt % 4 : mt % 4 + 2, cols], ADD)
+            nc.sync.dma_start(out_rows[:, mt : mt + 2, cols], results[b][:])

@@ -37,7 +37,6 @@ def tile_list_snapshot_finder_scores_kernel(
     with ExitStack() as ctx:
         lists = ctx.enter_context(tc.tile_pool(name="lists", bufs=1))
         keep = ctx.enter_context(tc.tile_pool(name="keep", bufs=1))
-        pair = ctx.enter_context(tc.tile_pool(name="pair", bufs=2))
         ring = ctx.enter_context(tc.tile_pool(name="ring", bufs=3))
         outs = ctx.enter_context(tc.tile_pool(name="outs", bufs=8))
         psum = ctx.enter_context(tc.psum_pool(name="psum", bufs=1))
@@ -59,14 +58,14 @@ def tile_list_snapshot_finder_scores_kernel(
             return tile
 
         def load_scales_side_by_side(queue, tile, src):
-            for q in range(4):
+            for r in range(4):
                 queue.dma_start(
-                    tile[32 * q : 32 * q + 4].bitcast(I32),
-                    src[:, 4 * q : 4 * q + 4, :].rearrange("a r n -> r a n").bitcast(I32),
+                    tile[r:P:32].bitcast(I32),
+                    src[:, r:16:4, :].rearrange("a q n -> q a n").bitcast(I32),
                 )
 
-        def load_weight(tag, src):
-            tile = pair.tile([P, PACK, BANK], F32, name=tag, align_bytes=64)
+        def load_weight(name, src):
+            tile = kept(name, [P, PACK, BANK], F32)
             nc.sync.dma_start(tile[:], src.rearrange("(p j) c -> p j c", j=PACK))
             return tile
 
@@ -95,24 +94,30 @@ def tile_list_snapshot_finder_scores_kernel(
         w2_raw = kept("w2_raw", [P, PASSES, 2 * R], U8)
         nc.sync.dma_start(w2_raw[:].bitcast(I32), w2_words.rearrange("a p n -> p a n").bitcast(I32))
         load_scales_side_by_side(nc.sync, w2_planes, w2_scales)
-        w1_raw = [load_weight("raw_a", w1[0:512, :])]
-        load_scales_side_by_side(nc.sync, tab_planes, tab_scales)
+        w1_raw = [load_weight("w1_raw0", w1[0:512, :])]
+        load_scales_side_by_side(nc.gpsimd, tab_planes, tab_scales)
         tab = [load_words("tab0", tab_words[0])]
-        w1_raw.append(load_weight("raw_a", w1[512:1024, :]))
+        w1_raw.append(load_weight("w1_raw1", w1[512:1024, :]))
         for q in range(4):
-            nc.sync.dma_start(
+            nc.gpsimd.dma_start(
                 tab2_planes[32 * q : 32 * q + 8, :].bitcast(I32),
                 tab2_scales[:, 4 * q : 4 * q + 4, :].bitcast(I32),
             )
         tab.append(load_words("tab1", tab_words[1]))
-        w3_raw = [load_weight("raw_b", w3[:, 0:512])]
+        w3_raw = [load_weight("w3_raw0", w3[:, 0:512])]
         tab2 = [load_words("tab2_0", tab2_words[0])]
         slots = load_list("slots", offs3)
         gains = kept("gains", [P, PASSES, PACK], F32)
         nc.sync.dma_start(gains[:], gain.rearrange("(a p t) -> p a t", a=PASSES, t=PACK))
-        wgs_dealt = kept("wgs_dealt", [P, PACK, S], F32)
-        for q in (0, 2, 1, 3):
-            nc.sync.dma_start(wgs_dealt[32 * q : 32 * q + 32], wgs.rearrange("(p t) j -> p t j", t=PACK))
+        wgs_rows = wgs.rearrange("(p t) j -> p t j", t=PACK)
+        wgs_dealt = []
+
+        def load_wgs(n):
+            t = len(wgs_dealt)
+            tile = kept("wgs%d" % t, [P, n, S], F32)
+            for q in (0, 2, 1, 3):
+                nc.sync.dma_start(tile[32 * q : 32 * q + 32], wgs_rows[:, t : t + n, :])
+            wgs_dealt.extend([tile[:, u, :] for u in range(n)])
 
         page_rows = page0.rearrange("(a p t) c -> a t p c", a=PASSES, t=PACK)
         pm_rows = pm.rearrange("(a p t) c -> a p t c", a=PASSES, t=PACK)
@@ -130,24 +135,28 @@ def tile_list_snapshot_finder_scores_kernel(
             nc.sync.dma_start(tile[:], pm_rows[i // PACK, :, i % PACK : i % PACK + n, :])
             pms.extend([tile[:, u, :] for u in range(n)])
 
+        load_wgs(1)
         load_page()
+        load_wgs(1)
         load_page()
         opened = load_list("opened", offs4)
         load_pm(1)
-        w3_raw.append(load_weight("raw_b", w3[:, 512:1024]))
+        load_wgs(2)
         load_page()
         load_pm(1)
-        for i in range(3, 7):
+        load_page()
+        w3_raw.append(load_weight("w3_raw1", w3[:, 512:1024]))
+        load_pm(1)
+        tab2.append(load_words("tab2_1", tab2_words[1]))
+        for i in range(4, 7):
             load_page()
             load_pm(1)
-            if i == 3:
-                tab2.append(load_words("tab2_1", tab2_words[1]))
         load_page()
         load_pm(2)
         dates_rows = dates.rearrange("(g m p) j -> g p m j", m=4, p=P)
         dates_sb = []
         for g in range(2):
-            tile = pair.tile([P, PACK, BANK], F32, name="raw_b", align_bytes=64)
+            tile = kept("dates%d" % g, [P, PACK, BANK], F32, "w3_raw%d" % g)
             nc.sync.dma_start(tile[:], dates_rows[g])
             dates_sb.append(tile)
 
@@ -254,10 +263,12 @@ def tile_list_snapshot_finder_scores_kernel(
             )
             if i == 0:
                 h = w3_grouped1[:].rearrange("p t m j -> p (t m j)").bitcast(F32)[:, 0:S]
+            elif i == 1:
+                h = w1_raw[0][:, 0, :]
             else:
                 h = ring.tile([P, S], F32, name="h")[:]
             nc.scalar.activation(h, acc[:], COPY, scale=gains[:, a, t : t + 1])
-            nc.vector.tensor_tensor(pages[i][:].indirect(slots[:]), h, wgs_dealt[:, t, :], MULT)
+            nc.vector.tensor_tensor(pages[i][:].indirect(slots[:]), h, wgs_dealt[t], MULT)
 
         def fetch(i, picked, cols):
             nc.vector.tensor_tensor(
@@ -276,19 +287,19 @@ def tile_list_snapshot_finder_scores_kernel(
 
         whole = slice(0, J)
         halves = [slice(0, HALF), slice(HALF, J)]
-        picked0 = pair.tile([P, PACK, J], F32, name="raw_a", align_bytes=64)
+        picked0 = kept("picked0", [P, PACK, J], F32, "w1_raw1")
         picked1 = [kept("picked1_%d" % u, [P, PACK, HALF], F32) for u in range(2)]
         nc.vector.tensor_copy(v2_codes[0][:], tab2[0][:].bitcast(U32).indirect(snaps[:]))
         put(0)
         put(1)
         fetch(0, picked0, whole)
-        w3_q.append(quantize_weight("w3_1", w3_grouped1, w3_raw[1]))
         put(2)
         fetch(1, picked0, whole)
-        v2_codes.append(kept("v2_codes1", [P, S2], U32))
-        nc.vector.tensor_copy(v2_codes[1][:], tab2[1][:].bitcast(U32).indirect(snaps[:]))
+        w3_q.append(quantize_weight("w3_1", w3_grouped1, w3_raw[1]))
         put(3)
         fetch(2, picked0, whole)
+        v2_codes.append(kept("v2_codes1", [P, S2], U32, "w1_raw0"))
+        nc.vector.tensor_copy(v2_codes[1][:], tab2[1][:].bitcast(U32).indirect(snaps[:]))
 
         tanh_f = kept("tanh_f", [P, S2 // P, J], F32)
         for mt in range(S2 // P):

@@ -37,12 +37,16 @@ def tile_list_snapshot_finder_scores_kernel(
     with ExitStack() as ctx:
         lists = ctx.enter_context(tc.tile_pool(name="lists", bufs=1))
         keep = ctx.enter_context(tc.tile_pool(name="keep", bufs=1))
+        early = ctx.enter_context(tc.tile_pool(name="early", bufs=1))
         ring = ctx.enter_context(tc.tile_pool(name="ring", bufs=3))
         outs = ctx.enter_context(tc.tile_pool(name="outs", bufs=8))
         psum = ctx.enter_context(tc.psum_pool(name="psum", bufs=1))
 
         def kept(name, shape, dtype, tag=None):
             return keep.tile(shape, dtype, name=name, tag=tag or name, align_bytes=64)
+
+        def placed(name, shape, dtype, offset):
+            return early.tile(shape, dtype, name=name, align_bytes=64, offset=offset)
 
         def bank(b):
             return psum.tile([P, BANK], F32, name="bank%d" % b)
@@ -64,47 +68,49 @@ def tile_list_snapshot_finder_scores_kernel(
                     src[:, r:16:4, :].rearrange("a q n -> q a n").bitcast(I32),
                 )
 
-        def load_weight(name, src):
-            tile = kept(name, [P, PACK, BANK], F32)
-            nc.sync.dma_start(tile[:], src.rearrange("(p j) c -> p j c", j=PACK))
-            return tile
-
         def quantize(codes, scales, values):
             nc.vector.quantize_mx(out=codes.bitcast(FP8X4), scales=scales, in_=values)
 
-        def quantize_weight(name, grouped, raw, reuse=None):
-            nc.scalar.copy(
-                grouped[:].rearrange("p t m j -> p m j t"),
-                raw[:].rearrange("p j (m t) -> p m j t", t=PACK),
-            )
-            codes = kept(name + "_codes", [P, BANK], U32, reuse)
+        def quantize_whole(name, grouped, codes):
             scales = kept(name + "_scales", [P, BANK], U8)
             quantize(codes[:], scales[:], grouped[:].rearrange("p t m j -> p (t m j)"))
             return codes, scales
 
-        tab_planes = kept("tab_planes", [P, PASSES, T], U8)
+        tab_planes = placed("tab_planes", [P, PASSES, T], U8, 2048)
         w2_planes = kept("w2_planes", [P, PASSES, R], U8)
         tab2_planes = kept("tab2_planes", [P, T3], U8)
-        for planes in (w2_planes, tab_planes, tab2_planes):
+        for planes in (tab_planes, w2_planes, tab2_planes):
             flat = planes[:] if len(planes.shape) == 2 else planes[:].rearrange("p a n -> p (a n)")
             nc.vector.memset(flat.bitcast(I32), 0)
 
+        w1_rows = w1.rearrange("(a p j) c -> a p j c", a=PASSES, j=PACK)
+        w1_raw = [kept("w1_raw%d" % a, [P, PACK, BANK], F32) for a in range(PASSES)]
+        nc.sync.dma_start(w1_raw[0][:], w1_rows[0])
         sites = load_list("sites", offs)
-        snaps = load_list("snaps", offs2)
+        load_scales_side_by_side(nc.gpsimd, tab_planes, tab_scales)
+        tab = [load_words("tab0", tab_words[0])]
         w2_raw = kept("w2_raw", [P, PASSES, 2 * R], U8)
         nc.sync.dma_start(w2_raw[:].bitcast(I32), w2_words.rearrange("a p n -> p a n").bitcast(I32))
         load_scales_side_by_side(nc.sync, w2_planes, w2_scales)
-        w1_raw = [load_weight("w1_raw0", w1[0:512, :])]
-        load_scales_side_by_side(nc.gpsimd, tab_planes, tab_scales)
-        tab = [load_words("tab0", tab_words[0])]
-        w1_raw.append(load_weight("w1_raw1", w1[512:1024, :]))
+        w1_late = w1_raw[1][:].rearrange("p j c -> p (j c)").rearrange("p (u j c) -> p u j c", u=2, j=PACK)
+        for u in range(2):
+            nc.sync.dma_start(w1_late[:, u], w1_rows[1][:, :, u * HALF : (u + 1) * HALF])
+        snaps = load_list("snaps", offs2)
         for q in range(4):
             nc.gpsimd.dma_start(
                 tab2_planes[32 * q : 32 * q + 8, :].bitcast(I32),
                 tab2_scales[:, 4 * q : 4 * q + 4, :].bitcast(I32),
             )
         tab.append(load_words("tab1", tab_words[1]))
-        w3_raw = [load_weight("w3_raw0", w3[:, 0:512])]
+        w3_rows = w3.rearrange("(g t i) c -> t g i c", t=PACK, i=8)
+
+        def load_w3(a):
+            tile = kept("w3_raw%d" % a, [P, PACK, BANK], F32)
+            for t in range(PACK):
+                nc.sync.dma_start(tile[:, t, :], w3_rows[t][:, :, a * BANK : (a + 1) * BANK])
+            return tile
+
+        w3_raw = [load_w3(0)]
         tab2 = [load_words("tab2_0", tab2_words[0])]
         slots = load_list("slots", offs3)
         gains = kept("gains", [P, PASSES, PACK], F32)
@@ -145,7 +151,7 @@ def tile_list_snapshot_finder_scores_kernel(
         load_page()
         load_pm(1)
         load_page()
-        w3_raw.append(load_weight("w3_raw1", w3[:, 512:1024]))
+        w3_raw.append(load_w3(1))
         load_pm(1)
         tab2.append(load_words("tab2_1", tab2_words[1]))
         for i in range(4, 7):
@@ -160,29 +166,43 @@ def tile_list_snapshot_finder_scores_kernel(
             nc.sync.dma_start(tile[:], dates_rows[g])
             dates_sb.append(tile)
 
-        w2_codes = kept("w2_codes", [P, PASSES, PACK, 2 * P], U8)
-        w2_dealt = kept("w2_dealt", [P, PASSES, PACK, P], U8)
+        w2_codes = placed("w2_codes", [P, PASSES, PACK, 2 * P], U8, 128)
+        w2_dealt = placed("w2_dealt", [P, PASSES, PACK, P], U8, 4224)
         v_scales = [kept("v_scales%d" % a, [P, S], U8) for a in range(PASSES)]
-        v_codes = [kept("v_codes0", [P, S], U32)]
-        nc.vector.tensor_copy(
-            w2_codes[:].bitcast(U16),
-            w2_raw[:].bitcast(U16).rearrange("p a (m t) -> p a t m", t=PACK),
-        )
-        nc.vector.tensor_copy(w2_dealt[:], w2_planes[:].rearrange("p a (m t) -> p a t m", t=PACK))
+        v_codes = [placed("v_codes0", [P, S], U32, 5248)]
         for a in range(PASSES):
             nc.vector.tensor_copy(v_scales[a][:], tab_planes[:, a, :].indirect(sites[:]))
-        w1_grouped0 = kept("w1_grouped0", GROUPED, BF16)
-        w1_q = [quantize_weight("w1_0", w1_grouped0, w1_raw[0], "tab_planes")]
+        w1_grouped = [kept("w1_grouped%d" % a, GROUPED, BF16) for a in range(PASSES)]
+        w1_grouped0 = w1_grouped[0]
+        nc.scalar.copy(
+            w1_grouped[0][:].rearrange("p t (g i) j -> p g t j i", i=8),
+            w1_raw[0][:].rearrange("p j (g t i) -> p g t j i", t=PACK, i=8),
+        )
+        w1_q = [quantize_whole("w1_0", w1_grouped[0], placed("w1_0_codes", [P, BANK], U32, 2176))]
         nc.vector.tensor_copy(v_codes[0][:], tab[0][:].bitcast(U32).indirect(sites[:]))
-        v2_scales = kept("v2_scales", [P, S2], U8)
-        nc.vector.tensor_copy(v2_scales[:], tab2_planes[:].indirect(snaps[:]))
-        w1_q.append(quantize_weight("w1_1", kept("w1_grouped1", GROUPED, BF16), w1_raw[1], "tab2_planes"))
+        nc.vector.tensor_copy(
+            w2_codes[:].bitcast(I32).rearrange("p a t (g w) -> p a t g w", w=4),
+            w2_raw[:].bitcast(I32).rearrange("p a (g t w) -> p a t g w", t=PACK, w=4),
+        )
+        nc.vector.tensor_copy(
+            w2_dealt[:].bitcast(I32).rearrange("p a t (g w) -> p a t g w", w=2),
+            w2_planes[:].bitcast(I32).rearrange("p a (g t w) -> p a t g w", t=PACK, w=2),
+        )
+        for u in range(2):
+            nc.scalar.copy(
+                w1_grouped[1][:].rearrange("p t (g i) j -> p g t j i", i=8)[:, 8 * u : 8 * (u + 1)],
+                w1_late[:, u].rearrange("p j (g t i) -> p g t j i", t=PACK, i=8),
+            )
+        w1_q.append(quantize_whole("w1_1", w1_grouped[1], kept("w1_1_codes", [P, BANK], U32, "tab0")))
         v_codes.append(kept("v_codes1", [P, S], U32, "w1_grouped1"))
         for u in range(2):
             nc.vector.tensor_copy(
                 v_codes[1][:, u * HALF : (u + 1) * HALF],
                 tab[1][:].bitcast(U32).indirect(sites[:, 16 * u : 16 * (u + 1)]),
             )
+
+        v2_scales = kept("v2_scales", [P, S2], U8, "tab1")
+        nc.vector.tensor_copy(v2_scales[:], tab2_planes[:].indirect(snaps[:]))
 
         n_chunks = S // CHUNK
         y1 = [bank(c) for c in range(n_chunks)]
@@ -218,7 +238,7 @@ def tile_list_snapshot_finder_scores_kernel(
             w2_products(1, c)
         b_codes = kept("b_codes", [P, S], U32)
         b_scales = kept("b_scales", [P, S], U8)
-        b_grouped = []
+        b_grouped = kept("b_grouped", [P, n_chunks, CHUNK, PACK], BF16, "tab2_planes")
         w3_halves = [
             w1_grouped0[:].rearrange("p t m j -> p (t m j)")[:, 0 : 2 * BANK],
             kept("w3_grouped0", [P, 2 * BANK], BF16)[:],
@@ -230,12 +250,10 @@ def tile_list_snapshot_finder_scores_kernel(
                 else:
                     y1_sb = kept("y1_sb%d" % c, [P, CHUNK, PACK], F32)[:]
                 nc.scalar.copy(y1_sb, y1[c][:].rearrange("p (t n) -> p n t", t=PACK))
-                grouped = kept("b_grouped%d" % c, [P, CHUNK, PACK], BF16)
-                nc.vector.tensor_tensor(grouped[:], y2[c][:].rearrange("p (t n) -> p n t", t=PACK), y1_sb, MAX)
-                b_grouped.append(grouped)
+                nc.vector.tensor_tensor(b_grouped[:, c], y2[c][:].rearrange("p (t n) -> p n t", t=PACK), y1_sb, MAX)
             if c > 0:
                 cols = slice((c - 1) * CHUNK, c * CHUNK)
-                quantize(b_codes[:, cols], b_scales[:, cols], b_grouped[c - 1][:].rearrange("p n t -> p (n t)"))
+                quantize(b_codes[:, cols], b_scales[:, cols], b_grouped[:, c - 1].rearrange("p n t -> p (n t)"))
 
 
         w3_q = [(kept("w3_0_codes", [P, BANK], U32), kept("w3_0_scales", [P, BANK], U8))]
@@ -295,7 +313,11 @@ def tile_list_snapshot_finder_scores_kernel(
         fetch(0, picked0, whole)
         put(2)
         fetch(1, picked0, whole)
-        w3_q.append(quantize_weight("w3_1", w3_grouped1, w3_raw[1]))
+        nc.scalar.copy(
+            w3_grouped1[:].rearrange("p t m j -> p m j t"),
+            w3_raw[1][:].rearrange("p j (m t) -> p m j t", t=PACK),
+        )
+        w3_q.append(quantize_whole("w3_1", w3_grouped1, kept("w3_1_codes", [P, BANK], U32)))
         put(3)
         fetch(2, picked0, whole)
         v2_codes.append(kept("v2_codes1", [P, S2], U32, "w1_raw0"))

from contextlib import ExitStack

import concourse.mybir as mybir

K, H, R, T, S, T2, S2, T3, J = 1024, 1024, 512, 2048, 512, 1024, 1024, 2048, 512
FLOPS = 2 * (2 * K * R * S + R * H * S + 2 * H * S2 * J)

F32 = mybir.dt.float32
BF16 = mybir.dt.bfloat16
I32 = mybir.dt.int32
U32 = mybir.dt.uint32
U16 = mybir.dt.uint16
U8 = mybir.dt.uint8
FP8X4 = mybir.dt.float8_e4m3fn_x4
FP4X4 = mybir.dt.float4_e2m1fn_x4
MULT = mybir.AluOpType.mult
ADD = mybir.AluOpType.add
MAX = mybir.AluOpType.max
COPY = mybir.ActivationFunctionType.Copy
TANH = mybir.ActivationFunctionType.Tanh

P = 128
PACK = 4
PASSES = 2
BANK = 512
CHUNK = 128
HALF = 256
GPSIMD_ADDS = 3
GROUPED = [P, PACK, P, PACK]


def tile_list_snapshot_finder_scores_kernel(
    tc, tab_words, tab_scales, offs, tab2_words, tab2_scales, offs2, offs3, offs4,
    w1, w2_words, w2_scales, w3, gain, wgs, page0, pm, dates, out,
):
    nc = tc.nc
    with ExitStack() as ctx:
        lists = ctx.enter_context(tc.tile_pool(name="lists", bufs=1))
        keep = ctx.enter_context(tc.tile_pool(name="keep", bufs=1))
        early = ctx.enter_context(tc.tile_pool(name="early", bufs=1))
        ring = ctx.enter_context(tc.tile_pool(name="ring", bufs=3))
        outs = ctx.enter_context(tc.tile_pool(name="outs", bufs=8))
        psum = ctx.enter_context(tc.psum_pool(name="psum", bufs=1))

        def kept(name, shape, dtype, tag=None):
            return keep.tile(shape, dtype, name=name, tag=tag or name, align_bytes=64)

        def placed(name, shape, dtype, offset):
            return early.tile(shape, dtype, name=name, align_bytes=64, offset=offset)

        def bank(b):
            return psum.tile([P, BANK], F32, name="bank%d" % b)

        def load_list(name, src):
            tile = lists.tile(list(src.shape), U16, name=name)
            nc.sync.dma_start(tile[:], src)
            return tile

        def load_words(name, src):
            tile = kept(name, [P, src.shape[1]], I32)
            nc.sync.dma_start(tile[:], src.rearrange("p t i -> p (t i)").bitcast(I32))
            return tile

        def load_scales_side_by_side(queue, tile, src):
            for r in range(4):
                queue.dma_start(
                    tile[r:P:32].bitcast(I32),
                    src[:, r:16:4, :].rearrange("a q n -> q a n").bitcast(I32),
                )

        def quantize(codes, scales, values):
            nc.vector.quantize_mx(out=codes.bitcast(FP8X4), scales=scales, in_=values)

        def quantize_whole(name, grouped, codes):
            scales = kept(name + "_scales", [P, BANK], U8)
            quantize(codes[:], scales[:], grouped[:].rearrange("p t m j -> p (t m j)"))
            return codes, scales

        tab_planes = placed("tab_planes", [P, PASSES, T], U8, 2048)
        w2_planes = kept("w2_planes", [P, PASSES, R], U8)
        tab2_planes = kept("tab2_planes", [P, T3], U8)
        for planes in (tab_planes, w2_planes, tab2_planes):
            flat = planes[:] if len(planes.shape) == 2 else planes[:].rearrange("p a n -> p (a n)")
            nc.vector.memset(flat.bitcast(I32), 0)

        w1_rows = w1.rearrange("(a p j) c -> a p j c", a=PASSES, j=PACK)
        w1_raw = [kept("w1_raw%d" % a, [P, PACK, BANK], F32) for a in range(PASSES)]
        nc.sync.dma_start(w1_raw[0][:], w1_rows[0])
        sites = load_list("sites", offs)
        load_scales_side_by_side(nc.gpsimd, tab_planes, tab_scales)
        tab = [load_words("tab0", tab_words[0])]
        w2_raw = kept("w2_raw", [P, PASSES, 2 * R], U8)
        nc.sync.dma_start(w2_raw[:].bitcast(I32), w2_words.rearrange("a p n -> p a n").bitcast(I32))
        load_scales_side_by_side(nc.sync, w2_planes, w2_scales)
        w1_late = w1_raw[1][:].rearrange("p j c -> p (j c)").rearrange("p (u j c) -> p u j c", u=2, j=PACK)
        for u in range(2):
            nc.sync.dma_start(w1_late[:, u], w1_rows[1][:, :, u * HALF : (u + 1) * HALF])
        snaps = load_list("snaps", offs2)
        for q in range(4):
            nc.gpsimd.dma_start(
                tab2_planes[32 * q : 32 * q + 8, :].bitcast(I32),
                tab2_scales[:, 4 * q : 4 * q + 4, :].bitcast(I32),
            )
        tab.append(load_words("tab1", tab_words[1]))
        w3_rows = w3.rearrange("(g t i) c -> t g i c", t=PACK, i=8)

        def load_w3(a):
            tile = kept("w3_raw%d" % a, [P, PACK, BANK], F32)
            for t in range(PACK):
                nc.sync.dma_start(tile[:, t, :], w3_rows[t][:, :, a * BANK : (a + 1) * BANK])
            return tile

        w3_raw = [load_w3(0)]
        tab2 = [load_words("tab2_0", tab2_words[0])]
        slots = load_list("slots", offs3)
        gains = kept("gains", [P, PASSES, PACK], F32)
        nc.sync.dma_start(gains[:], gain.rearrange("(a p t) -> p a t", a=PASSES, t=PACK))
        wgs_rows = wgs.rearrange("(p t) j -> p t j", t=PACK)
        wgs_dealt = []

        def load_wgs(n):
            t = len(wgs_dealt)
            tile = kept("wgs%d" % t, [P, n, S], F32)
            for q in (0, 2, 1, 3):
                nc.sync.dma_start(tile[32 * q : 32 * q + 32], wgs_rows[:, t : t + n, :])
            wgs_dealt.extend([tile[:, u, :] for u in range(n)])

        page_rows = page0.rearrange("(a p t) c -> a t p c", a=PASSES, t=PACK)
        pm_rows = pm.rearrange("(a p t) c -> a p t c", a=PASSES, t=PACK)
        pages, pms = [], []

        def load_page():
            i = len(pages)
            tile = kept("page%d" % i, [P, T2], F32)
            nc.sync.dma_start(tile[:], page_rows[i // PACK, i % PACK])
            pages.append(tile)

        def load_pm(n):
            i = len(pms)
            tile = kept("pm%d" % i, [P, n, J], F32)
            nc.sync.dma_start(tile[:], pm_rows[i // PACK, :, i % PACK : i % PACK + n, :])
            pms.extend([tile[:, u, :] for u in range(n)])

        load_wgs(1)
        load_page()
        load_wgs(1)
        load_page()
        opened = load_list("opened", offs4)
        load_pm(1)
        load_wgs(2)
        load_page()
        load_pm(1)
        load_page()
        w3_raw.append(load_w3(1))
        load_pm(1)
        tab2.append(load_words("tab2_1", tab2_words[1]))
        for i in range(4, 7):
            load_page()
            load_pm(1)
        load_page()
        load_pm(2)
        dates_rows = dates.rearrange("(g m p) j -> g p m j", m=4, p=P)
        dates_sb = []
        for g in range(2):
            tile = kept("dates%d" % g, [P, PACK, BANK], F32, "w3_raw%d" % g)
            nc.sync.dma_start(tile[:], dates_rows[g])
            dates_sb.append(tile)

        w2_codes = placed("w2_codes", [P, PASSES, PACK, 2 * P], U8, 128)
        w2_dealt = placed("w2_dealt", [P, PASSES, PACK, P], U8, 4224)
        v_scales = [kept("v_scales%d" % a, [P, S], U8) for a in range(PASSES)]
        v_codes = [placed("v_codes0", [P, S], U32, 5248)]
        for a in range(PASSES):
            nc.vector.tensor_copy(v_scales[a][:], tab_planes[:, a, :].indirect(sites[:]))
        w1_grouped = [kept("w1_grouped%d" % a, GROUPED, BF16) for a in range(PASSES)]
        w1_grouped0 = w1_grouped[0]
        nc.scalar.copy(
            w1_grouped[0][:].rearrange("p t (g i) j -> p g t j i", i=8),
            w1_raw[0][:].rearrange("p j (g t i) -> p g t j i", t=PACK, i=8),
        )
        w1_q = [quantize_whole("w1_0", w1_grouped[0], placed("w1_0_codes", [P, BANK], U32, 2176))]
        nc.vector.tensor_copy(v_codes[0][:], tab[0][:].bitcast(U32).indirect(sites[:]))
        nc.vector.tensor_copy(
            w2_codes[:].bitcast(I32).rearrange("p a t (g w) -> p a t g w", w=4),
            w2_raw[:].bitcast(I32).rearrange("p a (g t w) -> p a t g w", t=PACK, w=4),
        )
        nc.vector.tensor_copy(
            w2_dealt[:].bitcast(I32).rearrange("p a t (g w) -> p a t g w", w=2),
            w2_planes[:].bitcast(I32).rearrange("p a (g t w) -> p a t g w", t=PACK, w=2),
        )
        for u in range(2):
            nc.scalar.copy(
                w1_grouped[1][:].rearrange("p t (g i) j -> p g t j i", i=8)[:, 8 * u : 8 * (u + 1)],
                w1_late[:, u].rearrange("p j (g t i) -> p g t j i", t=PACK, i=8),
            )
        w1_q.append(quantize_whole("w1_1", w1_grouped[1], kept("w1_1_codes", [P, BANK], U32, "tab0")))
        v_codes.append(kept("v_codes1", [P, S], U32, "w1_grouped1"))
        for u in range(2):
            nc.vector.tensor_copy(
                v_codes[1][:, u * HALF : (u + 1) * HALF],
                tab[1][:].bitcast(U32).indirect(sites[:, 16 * u : 16 * (u + 1)]),
            )

        v2_scales = kept("v2_scales", [P, S2], U8, "tab1")
        nc.vector.tensor_copy(v2_scales[:], tab2_planes[:].indirect(snaps[:]))

        n_chunks = S // CHUNK
        y1 = [bank(c) for c in range(n_chunks)]
        y2 = [bank(n_chunks + c) for c in range(n_chunks)]

        def first_products(a, c, acc, weight, weight_scales):
            cols = slice(c * CHUNK, (c + 1) * CHUNK)
            for t in range(PACK):
                nc.tensor.matmul_mx(
                    out=acc[:, t * P : (t + 1) * P], lhsT=weight(a, t), lhsT_scale=weight_scales(a, t),
                    rhs=v_codes[a][:, cols].bitcast(FP8X4), rhs_scale=v_scales[a][:, cols],
                    start=(a == 0 and t == 0), stop=(a == PASSES - 1 and t == PACK - 1),
                )

        def w1_products(a, c):
            first_products(
                a, c, y1[c],
                lambda a, t: w1_q[a][0][:, t * P : (t + 1) * P].bitcast(FP8X4),
                lambda a, t: w1_q[a][1][:, t * P : (t + 1) * P],
            )

        def w2_products(a, c):
            first_products(
                a, c, y2[c], lambda a, t: w2_codes[:, a, t, :].bitcast(FP4X4), lambda a, t: w2_dealt[:, a, t, :]
            )

        for c in range(n_chunks):
            w1_products(0, c)
        for c in range(n_chunks):
            w2_products(0, c)
        for c in range(n_chunks):
            w1_products(1, c)
            w2_products(1, c)
        b_codes = kept("b_codes", [P, S], U32)
        b_scales = kept("b_scales", [P, S], U8)
        b_grouped = kept("b_grouped", [P, n_chunks, CHUNK, PACK], BF16, "tab2_planes")
        w3_halves = [
            w1_grouped0[:].rearrange("p t m j -> p (t m j)")[:, 0 : 2 * BANK],
            kept("w3_grouped0", [P, 2 * BANK], BF16)[:],
        ]
        for c in range(n_chunks + 1):
            if c < n_chunks:
                if c in (1, 2):
                    y1_sb = w3_halves[c - 1].bitcast(F32).rearrange("p (n t) -> p n t", t=PACK)
                else:
                    y1_sb = kept("y1_sb%d" % c, [P, CHUNK, PACK], F32)[:]
                nc.scalar.copy(y1_sb, y1[c][:].rearrange("p (t n) -> p n t", t=PACK))
                nc.vector.tensor_tensor(b_grouped[:, c], y2[c][:].rearrange("p (t n) -> p n t", t=PACK), y1_sb, MAX)
            if c > 0:
                cols = slice((c - 1) * CHUNK, c * CHUNK)
                quantize(b_codes[:, cols], b_scales[:, cols], b_grouped[:, c - 1].rearrange("p n t -> p (n t)"))


        w3_q = [(kept("w3_0_codes", [P, BANK], U32), kept("w3_0_scales", [P, BANK], U8))]
        for u in range(2):
            nc.scalar.copy(
                w3_halves[u].rearrange("p (t m j) -> p m j t", t=2, j=PACK),
                w3_raw[0][:].rearrange("p j (m t) -> p m j t", t=PACK)[:, :, :, 2 * u : 2 * u + 2],
            )
            cols = slice(u * HALF, (u + 1) * HALF)
            quantize(w3_q[0][0][:, cols], w3_q[0][1][:, cols], w3_halves[u])
        v2_codes = [kept("v2_codes0", [P, S2], U32, "w1_grouped0")]

        x_codes = [kept("x_codes%d" % a, [P, J], U32) for a in range(PASSES)]
        x_scales = [kept("x_scales%d" % a, [P, J], U8) for a in range(PASSES)]

        w3_grouped1 = kept("w3_grouped1", GROUPED, BF16)

        def put(i):
            a, t = divmod(i, PACK)
            m = slice(t * P, (t + 1) * P)
            acc = bank(i % 4)
            nc.tensor.matmul_mx(
                out=acc[:], lhsT=w3_q[a][0][:, m].bitcast(FP8X4), lhsT_scale=w3_q[a][1][:, m],
                rhs=b_codes[:].bitcast(FP8X4), rhs_scale=b_scales[:], start=True, stop=True,
            )
            if i == 0:
                h = w3_grouped1[:].rearrange("p t m j -> p (t m j)").bitcast(F32)[:, 0:S]
            elif i == 1:
                h = w1_raw[0][:, 0, :]
            else:
                h = ring.tile([P, S], F32, name="h")[:]
            nc.scalar.activation(h, acc[:], COPY, scale=gains[:, a, t : t + 1])
            nc.vector.tensor_tensor(pages[i][:].indirect(slots[:]), h, wgs_dealt[t], MULT)

        def fetch(i, picked, cols):
            nc.vector.tensor_tensor(
                picked[:, i % PACK, :],
                pages[i][:].indirect(opened[:, cols.start // 16 : cols.stop // 16]),
                pms[i][:, cols], MULT,
            )

        def quantize_x(a, picked, cols):
            grouped = kept("x_grouped%d_%d" % (a, cols.start), [P, cols.stop - cols.start, PACK], BF16)
            nc.scalar.copy(
                grouped[:].rearrange("p (c i) t -> p c t i", i=4),
                picked[:].rearrange("p t (c i) -> p c t i", i=4),
            )
            quantize(x_codes[a][:, cols], x_scales[a][:, cols], grouped[:].rearrange("p n t -> p (n t)"))

        whole = slice(0, J)
        halves = [slice(0, HALF), slice(HALF, J)]
        picked0 = kept("picked0", [P, PACK, J], F32, "w1_raw1")
        picked1 = [kept("picked1_%d" % u, [P, PACK, HALF], F32) for u in range(2)]
        nc.vector.tensor_copy(v2_codes[0][:], tab2[0][:].bitcast(U32).indirect(snaps[:]))
        put(0)
        put(1)
        fetch(0, picked0, whole)
        put(2)
        fetch(1, picked0, whole)
        nc.scalar.copy(
            w3_grouped1[:].rearrange("p t m j -> p m j t"),
            w3_raw[1][:].rearrange("p j (m t) -> p m j t", t=PACK),
        )
        w3_q.append(quantize_whole("w3_1", w3_grouped1, kept("w3_1_codes", [P, BANK], U32)))
        put(3)
        fetch(2, picked0, whole)
        v2_codes.append(kept("v2_codes1", [P, S2], U32, "w1_raw0"))
        nc.vector.tensor_copy(v2_codes[1][:], tab2[1][:].bitcast(U32).indirect(snaps[:]))

        tanh_f = kept("tanh_f", [P, S2 // P, J], F32)
        for mt in range(S2 // P):
            m = slice(mt * P, (mt + 1) * P)
            acc = bank(4 + mt % 4)
            for a in range(PASSES):
                nc.tensor.matmul_mx(
                    out=acc[:], lhsT=v2_codes[a][:, m].bitcast(FP8X4), lhsT_scale=v2_scales[4 * a :, m],
                    rhs=v_codes[a][:].bitcast(FP8X4), rhs_scale=v_scales[a][:],
                    start=(a == 0), stop=(a == PASSES - 1),
                )
            nc.scalar.activation(tanh_f[:, mt, :], acc[:], TANH)

        put(4)
        fetch(3, picked0, whole)
        quantize_x(0, picked0, whole)
        for i in (5, 6):
            put(i)
            for u in range(2):
                fetch(i - 1, picked1[u], halves[u])
        put(7)
        for u in range(2):
            fetch(6, picked1[u], halves[u])
            fetch(7, picked1[u], halves[u])
            quantize_x(1, picked1[u], halves[u])

        out_rows = out.rearrange("(m p) j -> p m j", p=P)
        e = [bank(b) for b in range(8)]
        for a in range(PASSES):
            for b in range(8):
                cols = halves[b // 4]
                for w in range(2):
                    mt = 2 * (b % 4) + w
                    m = slice(mt * P, (mt + 1) * P)
                    nc.tensor.matmul_mx(
                        out=e[b][:, w * HALF : (w + 1) * HALF],
                        lhsT=v2_codes[a][:, m].bitcast(FP8X4), lhsT_scale=v2_scales[4 * a :, m],
                        rhs=x_codes[a][:, cols].bitcast(FP8X4), rhs_scale=x_scales[a][:, cols],
                        start=(a == 0 and w == 0), stop=(a == PASSES - 1 and w == 1),
                    )
        results = []
        for b in range(8):
            cols = halves[b // 4]
            mt = 2 * (b % 4)
            result = outs.tile([P, 2, HALF], F32, name="result")
            nc.vector.tensor_tensor(
                result[:], e[b][:].rearrange("p (w n) -> p w n", w=2), tanh_f[:, mt : mt + 2, cols], MULT
            )
            results.append(result)
        for b in range(8):
            cols = halves[b // 4]
            mt = 2 * (b % 4)
            engine = nc.gpsimd if b < GPSIMD_ADDS else nc.vector
            engine.tensor_tensor(results[b][:], results[b][:], dates_sb[mt // 4][:, mt % 4 : mt % 4 + 2, cols], ADD)
            nc.sync.dma_start(out_rows[:, mt : mt + 2, cols], results[b][:])
